import numpy as np
import ml_dtypes


def mxq(x, axis, fmt="e4m3"):
    dtype, down = {"e4m3": (ml_dtypes.float8_e4m3fn, 7), "e5m2": (ml_dtypes.float8_e5m2, 14)}[fmt]
    v = np.moveaxis(np.asarray(x, np.float32).astype(ml_dtypes.bfloat16).astype(np.float64), axis, -1)
    blocks = v.reshape(v.shape[:-1] + (-1, 32))
    amax = np.abs(blocks).max(-1, keepdims=True)
    byte = np.maximum(np.where(amax > 0, np.frexp(amax)[1] - 1 + 127, 0) - down, 1)
    scale = np.exp2(byte - 127.0)
    codes = (blocks / scale).astype(np.float32).astype(dtype).astype(np.float64)
    return np.moveaxis((codes * scale).reshape(v.shape), -1, axis)


WIDE = False


def mx_kscale(k):
    if not WIDE:
        return np.ones(k)
    levels = np.array([30, -30])
    if k % 512:
        return np.exp2(np.random.permutation(np.resize(levels, k // 32))).repeat(32)
    a = np.empty((k // 512, 16))
    for p in range(k // 512):
        a[p, :8] = np.random.permutation(np.resize(levels, 8))
        for g in range(8):
            far = levels[np.abs(levels - a[p, g]) >= 10]
            a[p, g + 8] = far[np.random.randint(len(far))]
    return np.exp2(a.ravel()).repeat(32)


def f64(x):
    return np.asarray(x).astype(np.float64)


def striped(idx):
    return np.tile(np.asarray(idx).reshape(-1, 16).T, (8, 1)).astype(np.uint16)


def unstriped(offs):
    return offs[:16].T.reshape(-1).astype(np.int64)


E2M1 = np.array([0.0, 0.5, 1.0, 1.5, 2.0, 3.0, 4.0, 6.0, -0.0, -0.5, -1.0, -1.5, -2.0, -3.0, -4.0, -6.0])


def pack_weight(w, fmt):
    k, n = w.shape
    w = f64(np.asarray(w, np.float32).astype(ml_dtypes.bfloat16)).reshape(k // 32, 32, n)
    amax = np.abs(w).max(1)
    if fmt in ("e4m3", "e5m2"):
        byte = np.frexp(amax)[1] - 1 + 127 - (7 if fmt == "e4m3" else 14)
    else:
        mant, ex = np.frexp(amax / 6.0)
        byte = np.where(mant > 0.5, ex, ex - 1) + 127
    byte = np.clip(np.where(amax > 0, byte, 1), 1, 254)
    scaled = (w * np.exp2(127.0 - byte)[:, None, :]).reshape(k, n).astype(np.float32)
    by_word = np.ascontiguousarray(scaled.reshape(k // 512, 128, 4, n).transpose(0, 1, 3, 2))
    if fmt in ("e4m3", "e5m2"):
        words = by_word.astype(ml_dtypes.float8_e4m3fn if fmt == "e4m3" else ml_dtypes.float8_e5m2).view(np.uint8)
    else:
        c = by_word.astype(ml_dtypes.float4_e2m1fn).view(np.uint8) & 0xF
        words = (c[..., 0::2] | (c[..., 1::2] << 4)).reshape(k // 512, 128, 2 * n)
    return np.ascontiguousarray(words), np.ascontiguousarray(byte.astype(np.uint8).reshape(k // 512, 16, n))


def unpack_weight(words, scales, fmt):
    g, _, n = scales.shape
    words = np.ascontiguousarray(words).reshape(g, 128, n, -1)
    if fmt in ("e4m3", "e5m2"):
        vals = words.view(ml_dtypes.float8_e4m3fn if fmt == "e4m3" else ml_dtypes.float8_e5m2).astype(np.float64)
    else:
        nib = np.empty((g, 128, n, 4), np.uint8)
        nib[..., 0::2] = words & 0xF
        nib[..., 1::2] = words >> 4
        vals = E2M1[nib]
    vals = vals * np.repeat(np.exp2(scales.astype(np.float64) - 127.0), 8, axis=1)[..., None]
    return vals.transpose(0, 1, 3, 2).reshape(g * 512, n)


K, F, T, Z, J, R, O, N = 512, 512, 1024, 1024, 256, 512, 128, 256


def setup_inputs():
    n = np.random.standard_normal
    idx = np.random.permutation(T)[:J]
    idx2 = np.random.permutation(Z)[:J]
    idx3 = np.random.permutation(J)[:O]
    idx4 = np.random.permutation(J)[:O]
    idx5 = np.random.permutation(J)[:O]
    idx6 = np.random.permutation(T)[:O]
    fk = mx_kscale(K)
    fr = mx_kscale(R)
    ff = mx_kscale(F)
    xtp = pack_weight(n((K, T)) / fk[:, None], "e4m3")
    wp = pack_weight(n((K, R)) * 1 / np.sqrt(K) * fk[:, None] * fr, "e2m1")
    xop = pack_weight(n((F, Z)) / ff[:, None], "e2m1")
    w0p = pack_weight(n((F, R)) * 1 / np.sqrt(F) * ff[:, None] * fr, "e5m2")
    wbp = pack_weight(n((R, N)) * 1 / np.sqrt(R) / fr[:, None], "e5m2")
    wsp = pack_weight(n((K, N)) * 1 / np.sqrt(K) * fk[:, None], "e5m2")
    return {
        "xt_words": xtp[0],
        "xt_scales": xtp[1],
        "w_words": wp[0],
        "w_scales": wp[1],
        "xo_words": xop[0],
        "xo_scales": xop[1],
        "w0_words": w0p[0],
        "w0_scales": w0p[1],
        "wb_words": wbp[0],
        "wb_scales": wbp[1],
        "ws_words": wsp[0],
        "ws_scales": wsp[1],
        "offs": striped(idx),
        "offs2": striped(idx2),
        "offs3": striped(idx3),
        "offs4": striped(idx4),
        "offs5": striped(idx5),
        "offs6": striped(idx6),
    }


def reference(xt_words, xt_scales, w_words, w_scales, xo_words, xo_scales, w0_words, w0_scales, wb_words, wb_scales, ws_words, ws_scales, offs, offs2, offs3, offs4, offs5, offs6):
    idx = unstriped(offs)
    idx2 = unstriped(offs2)
    idx3 = unstriped(offs3)
    idx4 = unstriped(offs4)
    idx5 = unstriped(offs5)
    idx6 = unstriped(offs6)
    xtu = unpack_weight(xt_words, xt_scales, "e4m3")
    wu = unpack_weight(w_words, w_scales, "e2m1")
    xou = unpack_weight(xo_words, xo_scales, "e2m1")
    w0u = unpack_weight(w0_words, w0_scales, "e5m2")
    wbu = unpack_weight(wb_words, wb_scales, "e5m2")
    wsu = unpack_weight(ws_words, ws_scales, "e5m2")
    xtidxg = xtu[:, idx]
    xoidx2g = xou[:, idx2]
    a = wu.T @ xtidxg + w0u.T @ xoidx2g
    lo = np.minimum(a[:, idx3], a[:, idx4])
    hi = np.maximum(a[:, idx3], a[:, idx4])
    hid = np.maximum(lo, np.minimum(hi, a[:, idx5]))
    hidq = mxq(hid, 0, "e4m3")
    xtidx6g = xtu[:, idx6]
    y = wbu.T @ hidq + wsu.T @ xtidx6g
    return y

@@ -1,0 +1,212 @@
+from contextlib import ExitStack
+
+import concourse.mybir as mybir
+
+K, F, T, Z, J, R, O, N = 512, 512, 1024, 1024, 256, 512, 128, 256
+FLOPS = 2 * (K * R * J + F * R * J + R * N * O + K * N * O)
+
+F32 = mybir.dt.float32
+BF16 = mybir.dt.bfloat16
+I32 = mybir.dt.int32
+U32 = mybir.dt.uint32
+U16 = mybir.dt.uint16
+U8 = mybir.dt.uint8
+E4M3 = mybir.dt.float8_e4m3fn_x4
+E5M2 = mybir.dt.float8_e5m2_x4
+E2M1 = mybir.dt.float4_e2m1fn_x4
+MAX = mybir.AluOpType.max
+MIN = mybir.AluOpType.min
+COPY = mybir.ActivationFunctionType.Copy
+
+P = 128
+PACK = 4
+ROWS = 16
+
+
+def tile_list_middleofthree_bank_further_plain_kernel(
+    tc, xt_words, xt_scales, w_words, w_scales, xo_words, xo_scales, w0_words, w0_scales,
+    wb_words, wb_scales, ws_words, ws_scales, offs, offs2, offs3, offs4, offs5, offs6, out,
+):
+    nc = tc.nc
+    with ExitStack() as ctx:
+        sb = ctx.enter_context(tc.tile_pool(name="sb", bufs=1))
+        ps = ctx.enter_context(tc.psum_pool(name="ps", bufs=1))
+
+        def new(name, cols, dtype, tag=""):
+            return sb.tile([P, cols], dtype, name=name, tag=tag or name, align_bytes=64)
+
+        def load_list(name, src):
+            t = sb.tile([P, src.shape[1]], U16, name=name)
+            nc.sync.dma_start(t[:], src)
+            return t
+
+        def load_words8(queue, name, src, tag=""):
+            t = new(name, src.shape[2], I32, tag)
+            queue.dma_start(t[:], src[0].rearrange("p n b -> p (n b)").bitcast(I32))
+            return t
+
+        def load_words4(queue, name, src, tag=""):
+            t = new(name, src.shape[2] // 2, U16, tag)
+            queue.dma_start(t[:].bitcast(I32), src[0].bitcast(I32))
+            return t
+
+        def load_rows(queue, dst, src):
+            rows = src[0].bitcast(I32)
+            queue.dma_start(dst.bitcast(I32), rows.unsqueeze(1).to_broadcast([ROWS, P // ROWS, rows.shape[1]]))
+
+        def spread_rows(plane):
+            for r in range(1, 4):
+                nc.sync.dma_start(plane[r:P:32, :].bitcast(I32), plane[8 * r : P : 32, :].bitcast(I32))
+
+        xt_s = new("xt_s", T, U8)
+        xo_s = new("xo_s", Z, U8)
+        ww_s = new("ww_s", 2 * R, U8)
+        load_rows(nc.scalar, xt_s[:], xt_scales)
+        l1 = load_list("l1", offs)
+        load_rows(nc.scalar, xo_s[:], xo_scales)
+        l2 = load_list("l2", offs2)
+        load_rows(nc.scalar, ww_s[:, R : 2 * R], w0_scales)
+        load_rows(nc.sync, ww_s[:, 0:R], w_scales)
+        xt_w = load_words8(nc.sync, "xt_w", xt_words)
+        xo_w = load_words4(nc.scalar, "xo_w", xo_words)
+        l6 = load_list("l6", offs6)
+        w_w = load_words4(nc.sync, "w_w", w_words, "late_s")
+        w0_w = load_words8(nc.sync, "w0_w", w0_words, "late_w")
+        l3 = load_list("l3", offs3)
+        l4 = load_list("l4", offs4)
+        l5 = load_list("l5", offs5)
+
+        s1 = new("s1", 2 * J + 2 * R, U8)
+        xtg_r = new("xtg_r", J, U8)
+        nc.vector.tensor_copy(xtg_r[:], xt_s[:].indirect(l1[:]))
+        xog_r = new("xog_r", J, U8)
+        nc.vector.tensor_copy(xog_r[:], xo_s[:].indirect(l2[:]))
+        nc.vector.tensor_copy(s1[:, 0:J].bitcast(I32), xtg_r[:].bitcast(I32))
+        nc.vector.tensor_copy(
+            s1[:, 2 * J :].rearrange("p (h t m) -> p h t m", h=2, t=PACK),
+            ww_s[:].rearrange("p (h m t) -> p h t m", h=2, t=PACK),
+        )
+        nc.vector.tensor_copy(s1[:, J : 2 * J].bitcast(I32), xog_r[:].bitcast(I32))
+        spread_rows(s1)
+        xtg_s = s1[:, 0:J]
+        xog_s = s1[:, J : 2 * J]
+        wwp_s = s1[:, 2 * J :]
+
+        xtg_w = new("xtg_w", J, U32)
+        nc.vector.tensor_copy(xtg_w[:], xt_w[:].bitcast(U32).indirect(l1[:]))
+        xog_w = new("xog_w", J, U16)
+        nc.vector.tensor_copy(xog_w[:], xo_w[:].indirect(l2[:]))
+        wp_w = new("wp_w", R, U16)
+        nc.vector.tensor_copy(
+            wp_w[:].rearrange("p (t c i) -> p c t i", t=PACK, i=8),
+            w_w[:].rearrange("p (c i t) -> p c t i", t=PACK, i=8),
+        )
+        w0p_w = new("w0p_w", R, I32)
+        nc.vector.tensor_copy(
+            w0p_w[:].rearrange("p (t c i) -> p c t i", t=PACK, i=4),
+            w0_w[:].rearrange("p (c i t) -> p c t i", t=PACK, i=4),
+        )
+
+        s2 = new("s2", O + 2 * N, U8, "late_s")
+        load_rows(nc.sync, s2[:, O : O + N], ws_scales)
+        load_rows(nc.sync, s2[:, O + N :], wb_scales)
+        wsb_w = new("wsb_w", 2 * N, I32, "late_w")
+        ws_w = wsb_w[:, 0:N]
+        wb_w = wsb_w[:, N:]
+        nc.sync.dma_start(ws_w, ws_words[0].rearrange("p n b -> p (n b)").bitcast(I32))
+        nc.sync.dma_start(wb_w, wb_words[0].rearrange("p n b -> p (n b)").bitcast(I32))
+
+        a_ps = [ps.tile([P, J], F32, name="a_ps%d" % t) for t in range(PACK)]
+        for t in range(PACK):
+            cols = slice(t * P, (t + 1) * P)
+            nc.tensor.matmul_mx(
+                out=a_ps[t][:], lhsT=wp_w[:, cols].bitcast(E2M1), lhsT_scale=wwp_s[:, t * P : (t + 1) * P],
+                rhs=xtg_w[:].bitcast(E4M3), rhs_scale=xtg_s, start=True, stop=False,
+            )
+            nc.tensor.matmul_mx(
+                out=a_ps[t][:], lhsT=w0p_w[:, cols].bitcast(E5M2), lhsT_scale=wwp_s[:, R + t * P : R + (t + 1) * P],
+                rhs=xog_w[:].bitcast(E2M1), rhs_scale=xog_s, start=False, stop=True,
+            )
+
+        x6_r = new("x6_r", O, U8)
+        nc.vector.tensor_copy(x6_r[:], xt_s[:].indirect(l6[:]))
+        x6_w = new("x6_w", O, U32)
+        nc.vector.tensor_copy(x6_w[:], xt_w[:].bitcast(U32).indirect(l6[:]))
+        nc.vector.tensor_copy(s2[:, 0:O].bitcast(I32), x6_r[:].bitcast(I32))
+        spread_rows(s2)
+        x6_s = s2[:, 0:O]
+        ws_s = s2[:, O : O + N]
+        wb_s = s2[:, O + N :]
+        y_ps = [ps.tile([P, O], F32, name="y_ps%d" % h) for h in range(N // P)]
+        for h in range(N // P):
+            cols = slice(h * P, (h + 1) * P)
+            nc.tensor.matmul_mx(
+                out=y_ps[h][:], lhsT=ws_w[:, cols].bitcast(E5M2), lhsT_scale=ws_s[:, cols],
+                rhs=x6_w[:].bitcast(E4M3), rhs_scale=x6_s, start=True, stop=False,
+            )
+
+        g3 = new("g3", PACK * O, F32)
+        g4 = new("g4", PACK * O, F32)
+        g5 = new("g5", PACK * O, F32)
+        lo = new("lo", PACK * O, F32)
+        hi = new("hi", PACK * O, F32)
+        mid = new("mid", PACK * O, F32)
+        a_sb = [new("a_sb%d" % t, J, F32) for t in range(PACK)]
+
+        def minmax(cols):
+            nc.vector.tensor_tensor(hi[:, cols], g3[:, cols], g4[:, cols], MAX)
+            nc.vector.tensor_tensor(lo[:, cols], g3[:, cols], g4[:, cols], MIN)
+            nc.vector.tensor_tensor(mid[:, cols], hi[:, cols], g5[:, cols], MIN)
+
+        def pick(on_vector, dst, t, lst):
+            if on_vector:
+                nc.vector.tensor_copy(dst[:, t * O : (t + 1) * O], a_sb[t][:].indirect(lst[:]))
+            else:
+                nc.scalar.activation(dst[:, t * O : (t + 1) * O], a_sb[t][:].indirect(lst[:]), COPY)
+
+        nc.scalar.activation(a_sb[0][:], a_ps[0][:], COPY)
+        for t in range(2):
+            nc.scalar.activation(a_sb[t + 1][:], a_ps[t + 1][:], COPY)
+            pick(True, g3, t, l3)
+            pick(True, g4, t, l4)
+            pick(False, g5, t, l5)
+        nc.scalar.activation(a_sb[3][:], a_ps[3][:], COPY)
+        minmax(slice(0, 2 * O))
+        for t in range(2, PACK):
+            pick(False, g3, t, l3)
+            pick(False, g4, t, l4)
+            pick(t == 2, g5, t, l5)
+            minmax(slice(t * O, (t + 1) * O))
+
+        hid = new("hid", PACK * O, BF16)
+        hq_w = new("hq_w", O, U32)
+        hq_s = new("hq_s", O, U8)
+        half = O // 2
+        for u in range(2):
+            blk = slice(u * half // 4, (u + 1) * half // 4)
+            nc.vector.tensor_tensor(
+                hid[:].rearrange("p (c i t) -> p c t i", t=PACK, i=4)[:, blk],
+                lo[:].rearrange("p (t c i) -> p c t i", t=PACK, i=4)[:, blk],
+                mid[:].rearrange("p (t c i) -> p c t i", t=PACK, i=4)[:, blk],
+                MAX,
+            )
+        for u in range(2):
+            cols = slice(u * half, (u + 1) * half)
+            nc.vector.quantize_mx(
+                out=hq_w[:, cols].bitcast(E4M3), scales=hq_s[:, cols],
+                in_=hid[:, u * half * PACK : (u + 1) * half * PACK],
+            )
+
+        for h in range(N // P):
+            cols = slice(h * P, (h + 1) * P)
+            nc.tensor.matmul_mx(
+                out=y_ps[h][:], lhsT=wb_w[:, cols].bitcast(E5M2), lhsT_scale=wb_s[:, cols],
+                rhs=hq_w[:].bitcast(E4M3), rhs_scale=hq_s[:], start=False, stop=True,
+            )
+            y_sb = new("y_sb%d" % h, O, F32)
+            if h == 0:
+                nc.scalar.copy(y_sb[:], y_ps[h][:])
+                nc.scalar.dma_start(out[cols, :], y_sb[:])
+            else:
+                nc.vector.tensor_copy(y_sb[:], y_ps[h][:])
+                nc.sync.dma_start(out[cols, :], y_sb[:])

@@ -40,109 +40,117 @@ def tile_list_middleofthree_bank_further_plain_kernel(
             nc.sync.dma_start(t[:], src)
             return t
 
-        def load_words8(queue, name, src, tag=""):
-            t = new(name, src.shape[2], I32, tag)
-            queue.dma_start(t[:], src[0].rearrange("p n b -> p (n b)").bitcast(I32))
-            return t
+        def load_words8(queue, dst, src):
+            queue.dma_start(dst, src[0].rearrange("p n b -> p (n b)").bitcast(I32))
 
-        def load_words4(queue, name, src, tag=""):
-            t = new(name, src.shape[2] // 2, U16, tag)
-            queue.dma_start(t[:].bitcast(I32), src[0].bitcast(I32))
-            return t
+        def load_words4(queue, dst, src):
+            queue.dma_start(dst.bitcast(I32), src[0].bitcast(I32))
 
         def load_rows(queue, dst, src):
             rows = src[0].bitcast(I32)
             queue.dma_start(dst.bitcast(I32), rows.unsqueeze(1).to_broadcast([ROWS, P // ROWS, rows.shape[1]]))
 
-        def spread_rows(plane):
+        def place_rows(queues, plane):
             for r in range(1, 4):
-                nc.sync.dma_start(plane[r:P:32, :].bitcast(I32), plane[8 * r : P : 32, :].bitcast(I32))
+                queues[r - 1].dma_start(plane[r:P:32, :].bitcast(I32), plane[8 * r : P : 32, :].bitcast(I32))
+
+        def deal(dst, src, run, ts=slice(0, PACK)):
+            nc.vector.tensor_copy(
+                dst.rearrange("p (t c i) -> p c t i", t=ts.stop - ts.start, i=run),
+                src.rearrange("p (c i t) -> p c t i", t=PACK, i=run)[:, :, ts],
+            )
 
         xt_s = new("xt_s", T, U8)
         xo_s = new("xo_s", Z, U8)
-        ww_s = new("ww_s", 2 * R, U8)
+        w_s = new("w_s", R, U8)
+        w0_s = new("w0_s", R, U8)
+        xt_w = new("xt_w", T, I32)
+        xo_w = new("xo_w", Z, U16)
+        w_w = new("w_w", R, U16, "late_s")
+        w0_w = new("w0_w", R, I32, "late_w")
         load_rows(nc.scalar, xt_s[:], xt_scales)
         l1 = load_list("l1", offs)
+        load_rows(nc.sync, w_s[:], w_scales)
         load_rows(nc.scalar, xo_s[:], xo_scales)
         l2 = load_list("l2", offs2)
-        load_rows(nc.scalar, ww_s[:, R : 2 * R], w0_scales)
-        load_rows(nc.sync, ww_s[:, 0:R], w_scales)
-        xt_w = load_words8(nc.sync, "xt_w", xt_words)
-        xo_w = load_words4(nc.scalar, "xo_w", xo_words)
+        load_rows(nc.scalar, w0_s[:], w0_scales)
+        load_words4(nc.scalar, w_w[:], w_words)
+        load_words8(nc.sync, xt_w[:], xt_words)
+        load_words4(nc.sync, xo_w[:], xo_words)
+        load_words8(nc.sync, w0_w[:], w0_words)
+
+        def pick_rows(name, dst, table, lst):
+            picked = new(name, J, U8)
+            nc.vector.tensor_copy(picked[:], table[:].indirect(lst[:]))
+            return lambda: nc.vector.tensor_copy(dst.bitcast(I32), picked[:].bitcast(I32))
+
+        early = new("early", J + R // 2, U8)
+        late = new("late", J + R + R // 2, U8)
+        move = pick_rows("xt_picked", early[:, 0:J], xt_s, l1)
+        deal(early[:, J:], w_s[:], 16, slice(0, 2))
+        move()
+        place_rows((nc.scalar, nc.scalar, nc.scalar), early)
+        move = pick_rows("xo_picked", late[:, 0:J], xo_s, l2)
+        deal(late[:, J : J + R], w0_s[:], 16)
+        deal(late[:, J + R :], w_s[:], 16, slice(2, 4))
+        move()
+        place_rows((nc.sync, nc.scalar, nc.sync), late)
+        w_planes = [early[:, J : J + P], early[:, J + P :], late[:, J + R : J + R + P], late[:, J + R + P :]]
         l6 = load_list("l6", offs6)
-        w_w = load_words4(nc.sync, "w_w", w_words, "late_s")
-        w0_w = load_words8(nc.sync, "w0_w", w0_words, "late_w")
         l3 = load_list("l3", offs3)
         l4 = load_list("l4", offs4)
         l5 = load_list("l5", offs5)
 
-        s1 = new("s1", 2 * J + 2 * R, U8)
-        xtg_r = new("xtg_r", J, U8)
-        nc.vector.tensor_copy(xtg_r[:], xt_s[:].indirect(l1[:]))
-        xog_r = new("xog_r", J, U8)
-        nc.vector.tensor_copy(xog_r[:], xo_s[:].indirect(l2[:]))
-        nc.vector.tensor_copy(s1[:, 0:J].bitcast(I32), xtg_r[:].bitcast(I32))
-        nc.vector.tensor_copy(
-            s1[:, 2 * J :].rearrange("p (h t m) -> p h t m", h=2, t=PACK),
-            ww_s[:].rearrange("p (h m t) -> p h t m", h=2, t=PACK),
-        )
-        nc.vector.tensor_copy(s1[:, J : 2 * J].bitcast(I32), xog_r[:].bitcast(I32))
-        spread_rows(s1)
-        xtg_s = s1[:, 0:J]
-        xog_s = s1[:, J : 2 * J]
-        wwp_s = s1[:, 2 * J :]
-
         xtg_w = new("xtg_w", J, U32)
         nc.vector.tensor_copy(xtg_w[:], xt_w[:].bitcast(U32).indirect(l1[:]))
+        wp_w = new("wp_w", R, U16)
+        deal(wp_w[:], w_w[:], 8)
         xog_w = new("xog_w", J, U16)
         nc.vector.tensor_copy(xog_w[:], xo_w[:].indirect(l2[:]))
-        wp_w = new("wp_w", R, U16)
-        nc.vector.tensor_copy(
-            wp_w[:].rearrange("p (t c i) -> p c t i", t=PACK, i=8),
-            w_w[:].rearrange("p (c i t) -> p c t i", t=PACK, i=8),
-        )
         w0p_w = new("w0p_w", R, I32)
-        nc.vector.tensor_copy(
-            w0p_w[:].rearrange("p (t c i) -> p c t i", t=PACK, i=4),
-            w0_w[:].rearrange("p (c i t) -> p c t i", t=PACK, i=4),
-        )
+        deal(w0p_w[:], w0_w[:], 4)
 
-        s2 = new("s2", O + 2 * N, U8, "late_s")
-        load_rows(nc.sync, s2[:, O : O + N], ws_scales)
-        load_rows(nc.sync, s2[:, O + N :], wb_scales)
+        y_plane = new("y_plane", O + 2 * N, U8, "late_s")
+        load_rows(nc.sync, y_plane[:, O : O + N], ws_scales)
+        load_rows(nc.sync, y_plane[:, O + N :], wb_scales)
         wsb_w = new("wsb_w", 2 * N, I32, "late_w")
-        ws_w = wsb_w[:, 0:N]
-        wb_w = wsb_w[:, N:]
-        nc.sync.dma_start(ws_w, ws_words[0].rearrange("p n b -> p (n b)").bitcast(I32))
-        nc.sync.dma_start(wb_w, wb_words[0].rearrange("p n b -> p (n b)").bitcast(I32))
+        load_words8(nc.sync, wsb_w[:, 0:N], ws_words)
+        load_words8(nc.sync, wsb_w[:, N:], wb_words)
 
         a_ps = [ps.tile([P, J], F32, name="a_ps%d" % t) for t in range(PACK)]
-        for t in range(PACK):
-            cols = slice(t * P, (t + 1) * P)
+
+        def token_pass(t):
             nc.tensor.matmul_mx(
-                out=a_ps[t][:], lhsT=wp_w[:, cols].bitcast(E2M1), lhsT_scale=wwp_s[:, t * P : (t + 1) * P],
-                rhs=xtg_w[:].bitcast(E4M3), rhs_scale=xtg_s, start=True, stop=False,
-            )
-            nc.tensor.matmul_mx(
-                out=a_ps[t][:], lhsT=w0p_w[:, cols].bitcast(E5M2), lhsT_scale=wwp_s[:, R + t * P : R + (t + 1) * P],
-                rhs=xog_w[:].bitcast(E2M1), rhs_scale=xog_s, start=False, stop=True,
+                out=a_ps[t][:], lhsT=wp_w[:, t * P : (t + 1) * P].bitcast(E2M1),
+                lhsT_scale=w_planes[t],
+                rhs=xtg_w[:].bitcast(E4M3), rhs_scale=early[:, 0:J], start=True, stop=False,
             )
 
-        x6_r = new("x6_r", O, U8)
-        nc.vector.tensor_copy(x6_r[:], xt_s[:].indirect(l6[:]))
+        def note_pass(t):
+            nc.tensor.matmul_mx(
+                out=a_ps[t][:], lhsT=w0p_w[:, t * P : (t + 1) * P].bitcast(E5M2),
+                lhsT_scale=late[:, J + t * P : J + (t + 1) * P],
+                rhs=xog_w[:].bitcast(E2M1), rhs_scale=late[:, 0:J], start=False, stop=True,
+            )
+
+        for pair in range(0, PACK, 2):
+            token_pass(pair)
+            token_pass(pair + 1)
+            note_pass(pair)
+            note_pass(pair + 1)
+
+        x6_picked = new("x6_picked", O, U8)
+        nc.vector.tensor_copy(x6_picked[:], xt_s[:].indirect(l6[:]))
         x6_w = new("x6_w", O, U32)
         nc.vector.tensor_copy(x6_w[:], xt_w[:].bitcast(U32).indirect(l6[:]))
-        nc.vector.tensor_copy(s2[:, 0:O].bitcast(I32), x6_r[:].bitcast(I32))
-        spread_rows(s2)
-        x6_s = s2[:, 0:O]
-        ws_s = s2[:, O : O + N]
-        wb_s = s2[:, O + N :]
+        nc.vector.tensor_copy(y_plane[:, 0:O].bitcast(I32), x6_picked[:].bitcast(I32))
+        place_rows((nc.sync, nc.sync, nc.sync), y_plane)
         y_ps = [ps.tile([P, O], F32, name="y_ps%d" % h) for h in range(N // P)]
         for h in range(N // P):
-            cols = slice(h * P, (h + 1) * P)
             nc.tensor.matmul_mx(
-                out=y_ps[h][:], lhsT=ws_w[:, cols].bitcast(E5M2), lhsT_scale=ws_s[:, cols],
-                rhs=x6_w[:].bitcast(E4M3), rhs_scale=x6_s, start=True, stop=False,
+                out=y_ps[h][:], lhsT=wsb_w[:, h * P : (h + 1) * P].bitcast(E5M2),
+                lhsT_scale=y_plane[:, O + h * P : O + (h + 1) * P],
+                rhs=x6_w[:].bitcast(E4M3), rhs_scale=y_plane[:, 0:O], start=True, stop=False,
             )
 
         g3 = new("g3", PACK * O, F32)
@@ -153,30 +161,34 @@ def tile_list_middleofthree_bank_further_plain_kernel(
         mid = new("mid", PACK * O, F32)
         a_sb = [new("a_sb%d" % t, J, F32) for t in range(PACK)]
 
-        def minmax(cols):
-            nc.vector.tensor_tensor(hi[:, cols], g3[:, cols], g4[:, cols], MAX)
-            nc.vector.tensor_tensor(lo[:, cols], g3[:, cols], g4[:, cols], MIN)
-            nc.vector.tensor_tensor(mid[:, cols], hi[:, cols], g5[:, cols], MIN)
-
         def pick(on_vector, dst, t, lst):
             if on_vector:
                 nc.vector.tensor_copy(dst[:, t * O : (t + 1) * O], a_sb[t][:].indirect(lst[:]))
             else:
                 nc.scalar.activation(dst[:, t * O : (t + 1) * O], a_sb[t][:].indirect(lst[:]), COPY)
 
-        nc.scalar.activation(a_sb[0][:], a_ps[0][:], COPY)
+        def two(op, dst, x, y, t0, t1):
+            cols = slice(t0 * O, t1 * O)
+            nc.vector.tensor_tensor(dst[:, cols], x[:, cols], y[:, cols], op)
+
+        nc.vector.tensor_copy(a_sb[0][:], a_ps[0][:])
+        nc.scalar.activation(a_sb[1][:], a_ps[1][:], COPY)
         for t in range(2):
-            nc.scalar.activation(a_sb[t + 1][:], a_ps[t + 1][:], COPY)
             pick(True, g3, t, l3)
             pick(True, g4, t, l4)
             pick(False, g5, t, l5)
-        nc.scalar.activation(a_sb[3][:], a_ps[3][:], COPY)
-        minmax(slice(0, 2 * O))
+        for t in range(2, PACK):
+            nc.scalar.activation(a_sb[t][:], a_ps[t][:], COPY)
+        two(MAX, hi, g3, g4, 0, 2)
+        two(MIN, lo, g3, g4, 0, 2)
+        two(MIN, mid, hi, g5, 0, 2)
         for t in range(2, PACK):
             pick(False, g3, t, l3)
             pick(False, g4, t, l4)
             pick(t == 2, g5, t, l5)
-            minmax(slice(t * O, (t + 1) * O))
+            two(MAX, hi, g3, g4, t, t + 1)
+            two(MIN, lo, g3, g4, t, t + 1)
+            two(MIN, mid, hi, g5, t, t + 1)
 
         hid = new("hid", PACK * O, BF16)
         hq_w = new("hq_w", O, U32)
@@ -200,7 +212,8 @@ def tile_list_middleofthree_bank_further_plain_kernel(
         for h in range(N // P):
             cols = slice(h * P, (h + 1) * P)
             nc.tensor.matmul_mx(
-                out=y_ps[h][:], lhsT=wb_w[:, cols].bitcast(E5M2), lhsT_scale=wb_s[:, cols],
+                out=y_ps[h][:], lhsT=wsb_w[:, N + h * P : N + (h + 1) * P].bitcast(E5M2),
+                lhsT_scale=y_plane[:, O + N + h * P : O + N + (h + 1) * P],
                 rhs=hq_w[:].bitcast(E4M3), rhs_scale=hq_s[:], start=False, stop=True,
             )
             y_sb = new("y_sb%d" % h, O, F32)

@@ -20,7 +20,13 @@ COPY = mybir.ActivationFunctionType.Copy
 
 P = 128
 PACK = 4
-ROWS = 16
+BLOCKS = 16
+SPAN = P // BLOCKS
+QUADRANT = 32
+LINE = 16
+ENTRIES = 16
+HALF = O // 2
+FRONT, BACK = slice(0, 2), slice(2, 4)
 
 
 def tile_list_middleofthree_bank_further_plain_kernel(
@@ -36,29 +42,34 @@ def tile_list_middleofthree_bank_further_plain_kernel(
             return sb.tile([P, cols], dtype, name=name, tag=tag or name, align_bytes=64)
 
         def load_list(name, src):
-            t = sb.tile([P, src.shape[1]], U16, name=name)
-            nc.sync.dma_start(t[:], src)
-            return t
+            lst = sb.tile([P, src.shape[1]], U16, name=name)
+            nc.sync.dma_start(lst[:], src)
+            return lst
 
-        def load_words8(queue, dst, src):
+        def load_fp8_words(queue, dst, src):
             queue.dma_start(dst, src[0].rearrange("p n b -> p (n b)").bitcast(I32))
 
-        def load_words4(queue, dst, src):
+        def load_fp4_words(queue, dst, src):
             queue.dma_start(dst.bitcast(I32), src[0].bitcast(I32))
 
-        def load_rows(queue, dst, src):
+        def load_scale_rows(queue, dst, src):
             rows = src[0].bitcast(I32)
-            queue.dma_start(dst.bitcast(I32), rows.unsqueeze(1).to_broadcast([ROWS, P // ROWS, rows.shape[1]]))
+            queue.dma_start(dst.bitcast(I32), rows.unsqueeze(1).to_broadcast([BLOCKS, SPAN, rows.shape[1]]))
 
-        def place_rows(queues, plane):
-            for r in range(1, 4):
-                queues[r - 1].dma_start(plane[r:P:32, :].bitcast(I32), plane[8 * r : P : 32, :].bitcast(I32))
+        def place_scale_rows(queues, plane):
+            for s in range(1, PACK):
+                queues[s - 1].dma_start(
+                    plane[s:P:QUADRANT, :].bitcast(I32), plane[SPAN * s : P : QUADRANT, :].bitcast(I32)
+                )
 
-        def deal(dst, src, run, ts=slice(0, PACK)):
+        def deal(dst, src, run, tiles=slice(0, PACK)):
             nc.vector.tensor_copy(
-                dst.rearrange("p (t c i) -> p c t i", t=ts.stop - ts.start, i=run),
-                src.rearrange("p (c i t) -> p c t i", t=PACK, i=run)[:, :, ts],
+                dst.rearrange("p (t c i) -> p c t i", t=tiles.stop - tiles.start, i=run),
+                src.rearrange("p (c i t) -> p c t i", t=PACK, i=run)[:, :, tiles],
             )
+
+        def move_bytes(dst, src):
+            nc.vector.tensor_copy(dst.bitcast(I32), src.bitcast(I32))
 
         xt_s = new("xt_s", T, U8)
         xo_s = new("xo_s", Z, U8)
@@ -66,160 +77,153 @@ def tile_list_middleofthree_bank_further_plain_kernel(
         w0_s = new("w0_s", R, U8)
         xt_w = new("xt_w", T, I32)
         xo_w = new("xo_w", Z, U16)
-        w_w = new("w_w", R, U16, "late_s")
-        w0_w = new("w0_w", R, I32, "late_w")
-        load_rows(nc.scalar, xt_s[:], xt_scales)
-        l1 = load_list("l1", offs)
-        load_rows(nc.sync, w_s[:], w_scales)
-        load_rows(nc.scalar, xo_s[:], xo_scales)
-        l2 = load_list("l2", offs2)
-        load_rows(nc.scalar, w0_s[:], w0_scales)
-        load_words4(nc.scalar, w_w[:], w_words)
-        load_words8(nc.sync, xt_w[:], xt_words)
-        load_words4(nc.sync, xo_w[:], xo_words)
-        load_words8(nc.sync, w0_w[:], w0_words)
-
-        def pick_rows(name, dst, table, lst):
-            picked = new(name, J, U8)
-            nc.vector.tensor_copy(picked[:], table[:].indirect(lst[:]))
-            return lambda: nc.vector.tensor_copy(dst.bitcast(I32), picked[:].bitcast(I32))
+        w_w = new("w_w", R, U16, "w_words_then_y_plane")
+        w0_w = new("w0_w", R, I32, "w0_words_then_y_words")
+        load_scale_rows(nc.scalar, xt_s[:], xt_scales)
+        list1 = load_list("list1", offs)
+        load_scale_rows(nc.sync, w_s[:], w_scales)
+        load_scale_rows(nc.scalar, xo_s[:], xo_scales)
+        list2 = load_list("list2", offs2)
+        load_scale_rows(nc.scalar, w0_s[:], w0_scales)
+        load_fp4_words(nc.scalar, w_w[:], w_words)
+        load_fp8_words(nc.sync, xt_w[:], xt_words)
+        load_fp4_words(nc.sync, xo_w[:], xo_words)
+        load_fp8_words(nc.sync, w0_w[:], w0_words)
 
         early = new("early", J + R // 2, U8)
         late = new("late", J + R + R // 2, U8)
-        move = pick_rows("xt_picked", early[:, 0:J], xt_s, l1)
-        deal(early[:, J:], w_s[:], 16, slice(0, 2))
-        move()
-        place_rows((nc.scalar, nc.scalar, nc.scalar), early)
-        move = pick_rows("xo_picked", late[:, 0:J], xo_s, l2)
-        deal(late[:, J : J + R], w0_s[:], 16)
-        deal(late[:, J + R :], w_s[:], 16, slice(2, 4))
-        move()
-        place_rows((nc.sync, nc.scalar, nc.sync), late)
+        xt_picked_s = new("xt_picked_s", J, U8)
+        nc.vector.tensor_copy(xt_picked_s[:], xt_s[:].indirect(list1[:]))
+        deal(early[:, J:], w_s[:], LINE, FRONT)
+        move_bytes(early[:, 0:J], xt_picked_s[:])
+        place_scale_rows((nc.scalar, nc.scalar, nc.scalar), early)
+        xo_picked_s = new("xo_picked_s", J, U8)
+        nc.vector.tensor_copy(xo_picked_s[:], xo_s[:].indirect(list2[:]))
+        deal(late[:, J : J + R], w0_s[:], LINE)
+        deal(late[:, J + R :], w_s[:], LINE, BACK)
+        move_bytes(late[:, 0:J], xo_picked_s[:])
+        place_scale_rows((nc.sync, nc.scalar, nc.sync), late)
         w_planes = [early[:, J : J + P], early[:, J + P :], late[:, J + R : J + R + P], late[:, J + R + P :]]
-        l6 = load_list("l6", offs6)
-        l3 = load_list("l3", offs3)
-        l4 = load_list("l4", offs4)
-        l5 = load_list("l5", offs5)
+        list6 = load_list("list6", offs6)
+        list3 = load_list("list3", offs3)
+        list4 = load_list("list4", offs4)
+        list5 = load_list("list5", offs5)
 
-        xtg_w = new("xtg_w", J, U32)
-        nc.vector.tensor_copy(xtg_w[:], xt_w[:].bitcast(U32).indirect(l1[:]))
-        wp_w = new("wp_w", R, U16)
-        deal(wp_w[:], w_w[:], 8)
-        xog_w = new("xog_w", J, U16)
-        nc.vector.tensor_copy(xog_w[:], xo_w[:].indirect(l2[:]))
-        w0p_w = new("w0p_w", R, I32)
-        deal(w0p_w[:], w0_w[:], 4)
+        xt_picked_w = new("xt_picked_w", J, U32)
+        nc.vector.tensor_copy(xt_picked_w[:], xt_w[:].bitcast(U32).indirect(list1[:]))
+        w_dealt = new("w_dealt", R, U16)
+        deal(w_dealt[:], w_w[:], LINE // 2)
+        xo_picked_w = new("xo_picked_w", J, U16)
+        nc.vector.tensor_copy(xo_picked_w[:], xo_w[:].indirect(list2[:]))
+        w0_dealt = new("w0_dealt", R, I32)
+        deal(w0_dealt[:], w0_w[:], LINE // 4)
 
-        y_plane = new("y_plane", O + 2 * N, U8, "late_s")
-        load_rows(nc.sync, y_plane[:, O : O + N], ws_scales)
-        load_rows(nc.sync, y_plane[:, O + N :], wb_scales)
-        wsb_w = new("wsb_w", 2 * N, I32, "late_w")
-        load_words8(nc.sync, wsb_w[:, 0:N], ws_words)
-        load_words8(nc.sync, wsb_w[:, N:], wb_words)
+        y_plane = new("y_plane", O + 2 * N, U8, "w_words_then_y_plane")
+        load_scale_rows(nc.sync, y_plane[:, O : O + N], ws_scales)
+        load_scale_rows(nc.sync, y_plane[:, O + N :], wb_scales)
+        y_words = new("y_words", 2 * N, I32, "w0_words_then_y_words")
+        load_fp8_words(nc.sync, y_words[:, 0:N], ws_words)
+        load_fp8_words(nc.sync, y_words[:, N:], wb_words)
 
         a_ps = [ps.tile([P, J], F32, name="a_ps%d" % t) for t in range(PACK)]
+        for tiles in (FRONT, BACK):
+            for t in range(tiles.start, tiles.stop):
+                nc.tensor.matmul_mx(
+                    out=a_ps[t][:], lhsT=w_dealt[:, t * P : (t + 1) * P].bitcast(E2M1), lhsT_scale=w_planes[t],
+                    rhs=xt_picked_w[:].bitcast(E4M3), rhs_scale=early[:, 0:J], start=True, stop=False,
+                )
+            for t in range(tiles.start, tiles.stop):
+                nc.tensor.matmul_mx(
+                    out=a_ps[t][:], lhsT=w0_dealt[:, t * P : (t + 1) * P].bitcast(E5M2),
+                    lhsT_scale=late[:, J + t * P : J + (t + 1) * P],
+                    rhs=xo_picked_w[:].bitcast(E2M1), rhs_scale=late[:, 0:J], start=False, stop=True,
+                )
 
-        def token_pass(t):
-            nc.tensor.matmul_mx(
-                out=a_ps[t][:], lhsT=wp_w[:, t * P : (t + 1) * P].bitcast(E2M1),
-                lhsT_scale=w_planes[t],
-                rhs=xtg_w[:].bitcast(E4M3), rhs_scale=early[:, 0:J], start=True, stop=False,
-            )
-
-        def note_pass(t):
-            nc.tensor.matmul_mx(
-                out=a_ps[t][:], lhsT=w0p_w[:, t * P : (t + 1) * P].bitcast(E5M2),
-                lhsT_scale=late[:, J + t * P : J + (t + 1) * P],
-                rhs=xog_w[:].bitcast(E2M1), rhs_scale=late[:, 0:J], start=False, stop=True,
-            )
-
-        for pair in range(0, PACK, 2):
-            token_pass(pair)
-            token_pass(pair + 1)
-            note_pass(pair)
-            note_pass(pair + 1)
-
-        x6_picked = new("x6_picked", O, U8)
-        nc.vector.tensor_copy(x6_picked[:], xt_s[:].indirect(l6[:]))
-        x6_w = new("x6_w", O, U32)
-        nc.vector.tensor_copy(x6_w[:], xt_w[:].bitcast(U32).indirect(l6[:]))
-        nc.vector.tensor_copy(y_plane[:, 0:O].bitcast(I32), x6_picked[:].bitcast(I32))
-        place_rows((nc.sync, nc.sync, nc.sync), y_plane)
+        short_picked_s = new("short_picked_s", O, U8)
+        nc.vector.tensor_copy(short_picked_s[:], xt_s[:].indirect(list6[:]))
+        short_picked_w = new("short_picked_w", O, U32)
+        nc.vector.tensor_copy(short_picked_w[:], xt_w[:].bitcast(U32).indirect(list6[:]))
+        move_bytes(y_plane[:, 0:O], short_picked_s[:])
+        place_scale_rows((nc.sync, nc.sync, nc.sync), y_plane)
         y_ps = [ps.tile([P, O], F32, name="y_ps%d" % h) for h in range(N // P)]
         for h in range(N // P):
             nc.tensor.matmul_mx(
-                out=y_ps[h][:], lhsT=wsb_w[:, h * P : (h + 1) * P].bitcast(E5M2),
+                out=y_ps[h][:], lhsT=y_words[:, h * P : (h + 1) * P].bitcast(E5M2),
                 lhsT_scale=y_plane[:, O + h * P : O + (h + 1) * P],
-                rhs=x6_w[:].bitcast(E4M3), rhs_scale=y_plane[:, 0:O], start=True, stop=False,
+                rhs=short_picked_w[:].bitcast(E4M3), rhs_scale=y_plane[:, 0:O], start=True, stop=False,
             )
 
-        g3 = new("g3", PACK * O, F32)
-        g4 = new("g4", PACK * O, F32)
-        g5 = new("g5", PACK * O, F32)
+        first = new("first", PACK * O, F32)
+        second = new("second", PACK * O, F32)
+        third = new("third", PACK * O, F32)
         lo = new("lo", PACK * O, F32)
         hi = new("hi", PACK * O, F32)
-        mid = new("mid", PACK * O, F32)
+        capped = new("capped", PACK * O, F32)
         a_sb = [new("a_sb%d" % t, J, F32) for t in range(PACK)]
 
-        def pick(on_vector, dst, t, lst):
-            if on_vector:
-                nc.vector.tensor_copy(dst[:, t * O : (t + 1) * O], a_sb[t][:].indirect(lst[:]))
-            else:
-                nc.scalar.activation(dst[:, t * O : (t + 1) * O], a_sb[t][:].indirect(lst[:]), COPY)
+        def pick_operands(dst, t, lst, places):
+            offsets = lst[:, places.start // ENTRIES : places.stop // ENTRIES]
+            return dst[:, t * O + places.start : t * O + places.stop], a_sb[t][:].indirect(offsets)
 
-        def two(op, dst, x, y, t0, t1):
-            cols = slice(t0 * O, t1 * O)
-            nc.vector.tensor_tensor(dst[:, cols], x[:, cols], y[:, cols], op)
+        def pick_on_vector(dst, t, lst, places=slice(0, O)):
+            nc.vector.tensor_copy(*pick_operands(dst, t, lst, places))
 
+        def pick_on_scalar(dst, t, lst, places=slice(0, O)):
+            nc.scalar.activation(*pick_operands(dst, t, lst, places), COPY)
+
+        def combine(op, dst, x, y, tiles, places=slice(0, O)):
+            dst, x, y = (v[:].rearrange("p (t o) -> p t o", t=PACK)[:, tiles, places] for v in (dst, x, y))
+            nc.vector.tensor_tensor(dst, x, y, op)
+
+        lower, upper = slice(0, HALF), slice(HALF, O)
         nc.vector.tensor_copy(a_sb[0][:], a_ps[0][:])
         nc.scalar.activation(a_sb[1][:], a_ps[1][:], COPY)
-        for t in range(2):
-            pick(True, g3, t, l3)
-            pick(True, g4, t, l4)
-            pick(False, g5, t, l5)
-        for t in range(2, PACK):
+        pick_on_scalar(third, 0, list5)
+        for t in range(FRONT.start, FRONT.stop):
+            pick_on_vector(first, t, list3)
+            pick_on_vector(second, t, list4)
+        for t in range(BACK.start, BACK.stop):
             nc.scalar.activation(a_sb[t][:], a_ps[t][:], COPY)
-        two(MAX, hi, g3, g4, 0, 2)
-        two(MIN, lo, g3, g4, 0, 2)
-        two(MIN, mid, hi, g5, 0, 2)
-        for t in range(2, PACK):
-            pick(False, g3, t, l3)
-            pick(False, g4, t, l4)
-            pick(t == 2, g5, t, l5)
-            two(MAX, hi, g3, g4, t, t + 1)
-            two(MIN, lo, g3, g4, t, t + 1)
-            two(MIN, mid, hi, g5, t, t + 1)
+        combine(MAX, hi, first, second, FRONT)
+        combine(MIN, lo, first, second, FRONT)
+        pick_on_vector(third, 2, list5, lower)
+        for t in range(BACK.start, BACK.stop):
+            pick_on_scalar(first, t, list3)
+            pick_on_scalar(second, t, list4)
+            combine(MAX, hi, first, second, slice(t, t + 1))
+            combine(MIN, lo, first, second, slice(t, t + 1))
+        pick_on_scalar(third, 1, list5)
+        combine(MIN, capped, hi, third, FRONT)
+        pick_on_scalar(third, 3, list5, lower)
+        pick_on_scalar(third, 2, list5, upper)
+        pick_on_scalar(third, 3, list5, upper)
+        for places in (lower, upper):
+            combine(MIN, capped, hi, third, BACK, places)
 
         hid = new("hid", PACK * O, BF16)
-        hq_w = new("hq_w", O, U32)
-        hq_s = new("hq_s", O, U8)
-        half = O // 2
-        for u in range(2):
-            blk = slice(u * half // 4, (u + 1) * half // 4)
+        hid_w = new("hid_w", O, U32)
+        hid_s = new("hid_s", O, U8)
+        for places in (lower, upper):
+            pairs = slice(places.start // 2, places.stop // 2)
             nc.vector.tensor_tensor(
-                hid[:].rearrange("p (c i t) -> p c t i", t=PACK, i=4)[:, blk],
-                lo[:].rearrange("p (t c i) -> p c t i", t=PACK, i=4)[:, blk],
-                mid[:].rearrange("p (t c i) -> p c t i", t=PACK, i=4)[:, blk],
+                hid[:].rearrange("p (c i t) -> p c t i", t=PACK, i=2)[:, pairs],
+                lo[:].rearrange("p (t c i) -> p c t i", t=PACK, i=2)[:, pairs],
+                capped[:].rearrange("p (t c i) -> p c t i", t=PACK, i=2)[:, pairs],
                 MAX,
             )
-        for u in range(2):
-            cols = slice(u * half, (u + 1) * half)
+        for places in (lower, upper):
             nc.vector.quantize_mx(
-                out=hq_w[:, cols].bitcast(E4M3), scales=hq_s[:, cols],
-                in_=hid[:, u * half * PACK : (u + 1) * half * PACK],
+                out=hid_w[:, places].bitcast(E4M3), scales=hid_s[:, places],
+                in_=hid[:, places.start * PACK : places.stop * PACK],
             )
 
-        for h in range(N // P):
-            cols = slice(h * P, (h + 1) * P)
+        ends = ((nc.scalar.copy, nc.scalar), (nc.vector.tensor_copy, nc.sync))
+        for h, (empty, queue) in enumerate(ends):
             nc.tensor.matmul_mx(
-                out=y_ps[h][:], lhsT=wsb_w[:, N + h * P : N + (h + 1) * P].bitcast(E5M2),
+                out=y_ps[h][:], lhsT=y_words[:, N + h * P : N + (h + 1) * P].bitcast(E5M2),
                 lhsT_scale=y_plane[:, O + N + h * P : O + N + (h + 1) * P],
-                rhs=hq_w[:].bitcast(E4M3), rhs_scale=hq_s[:], start=False, stop=True,
+                rhs=hid_w[:].bitcast(E4M3), rhs_scale=hid_s[:], start=False, stop=True,
             )
             y_sb = new("y_sb%d" % h, O, F32)
-            if h == 0:
-                nc.scalar.copy(y_sb[:], y_ps[h][:])
-                nc.scalar.dma_start(out[cols, :], y_sb[:])
-            else:
-                nc.vector.tensor_copy(y_sb[:], y_ps[h][:])
-                nc.sync.dma_start(out[cols, :], y_sb[:])
+            empty(y_sb[:], y_ps[h][:])
+            queue.dma_start(out[h * P : (h + 1) * P, :], y_sb[:])

from contextlib import ExitStack

import concourse.mybir as mybir

K, F, T, Z, J, R, O, N = 512, 512, 1024, 1024, 256, 512, 128, 256
FLOPS = 2 * (K * R * J + F * R * J + R * N * O + K * N * O)

F32 = mybir.dt.float32
BF16 = mybir.dt.bfloat16
I32 = mybir.dt.int32
U32 = mybir.dt.uint32
U16 = mybir.dt.uint16
U8 = mybir.dt.uint8
E4M3 = mybir.dt.float8_e4m3fn_x4
E5M2 = mybir.dt.float8_e5m2_x4
E2M1 = mybir.dt.float4_e2m1fn_x4
MAX = mybir.AluOpType.max
MIN = mybir.AluOpType.min
COPY = mybir.ActivationFunctionType.Copy

P = 128
PACK = 4
BLOCKS = 16
SPAN = P // BLOCKS
QUADRANT = 32
LINE = 16
ENTRIES = 16
HALF = O // 2
FRONT, BACK = slice(0, 2), slice(2, 4)


def tile_list_middleofthree_bank_further_plain_kernel(
    tc, xt_words, xt_scales, w_words, w_scales, xo_words, xo_scales, w0_words, w0_scales,
    wb_words, wb_scales, ws_words, ws_scales, offs, offs2, offs3, offs4, offs5, offs6, out,
):
    nc = tc.nc
    with ExitStack() as ctx:
        sb = ctx.enter_context(tc.tile_pool(name="sb", bufs=1))
        ps = ctx.enter_context(tc.psum_pool(name="ps", bufs=1))

        def new(name, cols, dtype, tag=""):
            return sb.tile([P, cols], dtype, name=name, tag=tag or name, align_bytes=64)

        def load_list(name, src):
            lst = sb.tile([P, src.shape[1]], U16, name=name)
            nc.sync.dma_start(lst[:], src)
            return lst

        def load_fp8_words(queue, dst, src):
            queue.dma_start(dst, src[0].rearrange("p n b -> p (n b)").bitcast(I32))

        def load_fp4_words(queue, dst, src):
            queue.dma_start(dst.bitcast(I32), src[0].bitcast(I32))

        def load_scale_rows(queue, dst, src):
            rows = src[0].bitcast(I32)
            queue.dma_start(dst.bitcast(I32), rows.unsqueeze(1).to_broadcast([BLOCKS, SPAN, rows.shape[1]]))

        def place_scale_rows(queues, plane):
            for s in range(1, PACK):
                queues[s - 1].dma_start(
                    plane[s:P:QUADRANT, :].bitcast(I32), plane[SPAN * s : P : QUADRANT, :].bitcast(I32)
                )

        def deal(dst, src, run, tiles=slice(0, PACK)):
            nc.vector.tensor_copy(
                dst.rearrange("p (t c i) -> p c t i", t=tiles.stop - tiles.start, i=run),
                src.rearrange("p (c i t) -> p c t i", t=PACK, i=run)[:, :, tiles],
            )

        def move_bytes(dst, src):
            nc.vector.tensor_copy(dst.bitcast(I32), src.bitcast(I32))

        xt_s = new("xt_s", T, U8)
        xo_s = new("xo_s", Z, U8)
        w_s = new("w_s", R, U8)
        w0_s = new("w0_s", R, U8)
        xt_w = new("xt_w", T, I32)
        xo_w = new("xo_w", Z, U16)
        w_w = new("w_w", R, U16, "w_words_then_y_plane")
        w0_w = new("w0_w", R, I32, "w0_words_then_y_words")
        load_scale_rows(nc.scalar, xt_s[:], xt_scales)
        list1 = load_list("list1", offs)
        load_scale_rows(nc.sync, w_s[:], w_scales)
        load_scale_rows(nc.scalar, xo_s[:], xo_scales)
        list2 = load_list("list2", offs2)
        load_scale_rows(nc.scalar, w0_s[:], w0_scales)
        load_fp4_words(nc.scalar, w_w[:], w_words)
        load_fp8_words(nc.sync, xt_w[:], xt_words)
        load_fp4_words(nc.sync, xo_w[:], xo_words)
        load_fp8_words(nc.sync, w0_w[:], w0_words)

        early = new("early", J + R // 2, U8)
        late = new("late", J + R + R // 2, U8)
        xt_picked_s = new("xt_picked_s", J, U8)
        nc.vector.tensor_copy(xt_picked_s[:], xt_s[:].indirect(list1[:]))
        deal(early[:, J:], w_s[:], LINE, FRONT)
        move_bytes(early[:, 0:J], xt_picked_s[:])
        place_scale_rows((nc.scalar, nc.scalar, nc.scalar), early)
        xo_picked_s = new("xo_picked_s", J, U8)
        nc.vector.tensor_copy(xo_picked_s[:], xo_s[:].indirect(list2[:]))
        deal(late[:, J : J + R], w0_s[:], LINE)
        deal(late[:, J + R :], w_s[:], LINE, BACK)
        move_bytes(late[:, 0:J], xo_picked_s[:])
        place_scale_rows((nc.sync, nc.scalar, nc.sync), late)
        w_planes = [early[:, J : J + P], early[:, J + P :], late[:, J + R : J + R + P], late[:, J + R + P :]]
        list6 = load_list("list6", offs6)
        list3 = load_list("list3", offs3)
        list4 = load_list("list4", offs4)
        list5 = load_list("list5", offs5)

        xt_picked_w = new("xt_picked_w", J, U32)
        nc.vector.tensor_copy(xt_picked_w[:], xt_w[:].bitcast(U32).indirect(list1[:]))
        w_dealt = new("w_dealt", R, U16)
        deal(w_dealt[:], w_w[:], LINE // 2)
        xo_picked_w = new("xo_picked_w", J, U16)
        nc.vector.tensor_copy(xo_picked_w[:], xo_w[:].indirect(list2[:]))
        w0_dealt = new("w0_dealt", R, I32)
        deal(w0_dealt[:], w0_w[:], LINE // 4)

        y_plane = new("y_plane", O + 2 * N, U8, "w_words_then_y_plane")
        load_scale_rows(nc.sync, y_plane[:, O : O + N], ws_scales)
        load_scale_rows(nc.sync, y_plane[:, O + N :], wb_scales)
        y_words = new("y_words", 2 * N, I32, "w0_words_then_y_words")
        load_fp8_words(nc.sync, y_words[:, 0:N], ws_words)
        load_fp8_words(nc.sync, y_words[:, N:], wb_words)

        a_ps = [ps.tile([P, J], F32, name="a_ps%d" % t) for t in range(PACK)]
        for tiles in (FRONT, BACK):
            for t in range(tiles.start, tiles.stop):
                nc.tensor.matmul_mx(
                    out=a_ps[t][:], lhsT=w_dealt[:, t * P : (t + 1) * P].bitcast(E2M1), lhsT_scale=w_planes[t],
                    rhs=xt_picked_w[:].bitcast(E4M3), rhs_scale=early[:, 0:J], start=True, stop=False,
                )
            for t in range(tiles.start, tiles.stop):
                nc.tensor.matmul_mx(
                    out=a_ps[t][:], lhsT=w0_dealt[:, t * P : (t + 1) * P].bitcast(E5M2),
                    lhsT_scale=late[:, J + t * P : J + (t + 1) * P],
                    rhs=xo_picked_w[:].bitcast(E2M1), rhs_scale=late[:, 0:J], start=False, stop=True,
                )

        short_picked_s = new("short_picked_s", O, U8)
        nc.vector.tensor_copy(short_picked_s[:], xt_s[:].indirect(list6[:]))
        short_picked_w = new("short_picked_w", O, U32)
        nc.vector.tensor_copy(short_picked_w[:], xt_w[:].bitcast(U32).indirect(list6[:]))
        move_bytes(y_plane[:, 0:O], short_picked_s[:])
        place_scale_rows((nc.sync, nc.sync, nc.sync), y_plane)
        y_ps = [ps.tile([P, O], F32, name="y_ps%d" % h) for h in range(N // P)]
        for h in range(N // P):
            nc.tensor.matmul_mx(
                out=y_ps[h][:], lhsT=y_words[:, h * P : (h + 1) * P].bitcast(E5M2),
                lhsT_scale=y_plane[:, O + h * P : O + (h + 1) * P],
                rhs=short_picked_w[:].bitcast(E4M3), rhs_scale=y_plane[:, 0:O], start=True, stop=False,
            )

        first = new("first", PACK * O, F32)
        second = new("second", PACK * O, F32)
        third = new("third", PACK * O, F32)
        lo = new("lo", PACK * O, F32)
        hi = new("hi", PACK * O, F32)
        capped = new("capped", PACK * O, F32)
        a_sb = [new("a_sb%d" % t, J, F32) for t in range(PACK)]

        def pick_operands(dst, t, lst, places):
            offsets = lst[:, places.start // ENTRIES : places.stop // ENTRIES]
            return dst[:, t * O + places.start : t * O + places.stop], a_sb[t][:].indirect(offsets)

        def pick_on_vector(dst, t, lst, places=slice(0, O)):
            nc.vector.tensor_copy(*pick_operands(dst, t, lst, places))

        def pick_on_scalar(dst, t, lst, places=slice(0, O)):
            nc.scalar.activation(*pick_operands(dst, t, lst, places), COPY)

        def combine(op, dst, x, y, tiles, places=slice(0, O)):
            dst, x, y = (v[:].rearrange("p (t o) -> p t o", t=PACK)[:, tiles, places] for v in (dst, x, y))
            nc.vector.tensor_tensor(dst, x, y, op)

        lower, upper = slice(0, HALF), slice(HALF, O)
        nc.vector.tensor_copy(a_sb[0][:], a_ps[0][:])
        nc.scalar.activation(a_sb[1][:], a_ps[1][:], COPY)
        pick_on_scalar(third, 0, list5)
        for t in range(FRONT.start, FRONT.stop):
            pick_on_vector(first, t, list3)
            pick_on_vector(second, t, list4)
        for t in range(BACK.start, BACK.stop):
            nc.scalar.activation(a_sb[t][:], a_ps[t][:], COPY)
        combine(MAX, hi, first, second, FRONT)
        combine(MIN, lo, first, second, FRONT)
        pick_on_vector(third, 2, list5, lower)
        for t in range(BACK.start, BACK.stop):
            pick_on_scalar(first, t, list3)
            pick_on_scalar(second, t, list4)
            combine(MAX, hi, first, second, slice(t, t + 1))
            combine(MIN, lo, first, second, slice(t, t + 1))
        pick_on_scalar(third, 1, list5)
        combine(MIN, capped, hi, third, FRONT)
        pick_on_scalar(third, 3, list5, lower)
        pick_on_scalar(third, 2, list5, upper)
        pick_on_scalar(third, 3, list5, upper)
        for places in (lower, upper):
            combine(MIN, capped, hi, third, BACK, places)

        hid = new("hid", PACK * O, BF16)
        hid_w = new("hid_w", O, U32)
        hid_s = new("hid_s", O, U8)
        for places in (lower, upper):
            pairs = slice(places.start // 2, places.stop // 2)
            nc.vector.tensor_tensor(
                hid[:].rearrange("p (c i t) -> p c t i", t=PACK, i=2)[:, pairs],
                lo[:].rearrange("p (t c i) -> p c t i", t=PACK, i=2)[:, pairs],
                capped[:].rearrange("p (t c i) -> p c t i", t=PACK, i=2)[:, pairs],
                MAX,
            )
        for places in (lower, upper):
            nc.vector.quantize_mx(
                out=hid_w[:, places].bitcast(E4M3), scales=hid_s[:, places],
                in_=hid[:, places.start * PACK : places.stop * PACK],
            )

        ends = ((nc.scalar.copy, nc.scalar), (nc.vector.tensor_copy, nc.sync))
        for h, (empty, queue) in enumerate(ends):
            nc.tensor.matmul_mx(
                out=y_ps[h][:], lhsT=y_words[:, N + h * P : N + (h + 1) * P].bitcast(E5M2),
                lhsT_scale=y_plane[:, O + N + h * P : O + N + (h + 1) * P],
                rhs=hid_w[:].bitcast(E4M3), rhs_scale=hid_s[:], start=False, stop=True,
            )
            y_sb = new("y_sb%d" % h, O, F32)
            empty(y_sb[:], y_ps[h][:])
            queue.dma_start(out[h * P : (h + 1) * P, :], y_sb[:])
